import numpy as np
import ml_dtypes


def mxq(x, axis, fmt="e4m3"):
    dtype, down = {"e4m3": (ml_dtypes.float8_e4m3fn, 7), "e5m2": (ml_dtypes.float8_e5m2, 14)}[fmt]
    v = np.moveaxis(np.asarray(x, np.float32).astype(ml_dtypes.bfloat16).astype(np.float64), axis, -1)
    blocks = v.reshape(v.shape[:-1] + (-1, 32))
    amax = np.abs(blocks).max(-1, keepdims=True)
    byte = np.maximum(np.where(amax > 0, np.frexp(amax)[1] - 1 + 127, 0) - down, 1)
    scale = np.exp2(byte - 127.0)
    codes = (blocks / scale).astype(np.float32).astype(dtype).astype(np.float64)
    return np.moveaxis((codes * scale).reshape(v.shape), -1, axis)


WIDE = False


def mx_kscale(k):
    if not WIDE:
        return np.ones(k)
    levels = np.array([10, -10, 5, -5, 0])
    if k % 512:
        return np.exp2(np.random.permutation(np.resize(levels, k // 32))).repeat(32)
    a = np.empty((k // 512, 16))
    for p in range(k // 512):
        a[p, :8] = np.random.permutation(np.resize(levels, 8))
        for g in range(8):
            far = levels[np.abs(levels - a[p, g]) >= 10]
            a[p, g + 8] = far[np.random.randint(len(far))]
    return np.exp2(a.ravel()).repeat(32)


def f64(x):
    return np.asarray(x).astype(np.float64)


def striped(idx):
    return np.tile(np.asarray(idx).reshape(-1, 16).T, (8, 1)).astype(np.uint16)


def unstriped(offs):
    return offs[:16].T.reshape(-1).astype(np.int64)


E2M1 = np.array([0.0, 0.5, 1.0, 1.5, 2.0, 3.0, 4.0, 6.0, -0.0, -0.5, -1.0, -1.5, -2.0, -3.0, -4.0, -6.0])


def pack_weight(w, fmt):
    k, n = w.shape
    w = f64(np.asarray(w, np.float32).astype(ml_dtypes.bfloat16)).reshape(k // 32, 32, n)
    amax = np.abs(w).max(1)
    if fmt == "e4m3":
        byte = np.frexp(amax)[1] - 1 + 127 - 7
    else:
        mant, ex = np.frexp(amax / 6.0)
        byte = np.where(mant > 0.5, ex, ex - 1) + 127
    byte = np.clip(np.where(amax > 0, byte, 1), 1, 254)
    scaled = (w * np.exp2(127.0 - byte)[:, None, :]).reshape(k, n).astype(np.float32)
    by_word = np.ascontiguousarray(scaled.reshape(k // 512, 128, 4, n).transpose(0, 1, 3, 2))
    if fmt == "e4m3":
        words = by_word.astype(ml_dtypes.float8_e4m3fn).view(np.uint8)
    else:
        c = by_word.astype(ml_dtypes.float4_e2m1fn).view(np.uint8) & 0xF
        words = (c[..., 0::2] | (c[..., 1::2] << 4)).reshape(k // 512, 128, 2 * n)
    return np.ascontiguousarray(words), np.ascontiguousarray(byte.astype(np.uint8).reshape(k // 512, 16, n))


def unpack_weight(words, scales, fmt):
    g, _, n = scales.shape
    words = np.ascontiguousarray(words).reshape(g, 128, n, -1)
    if fmt == "e4m3":
        vals = words.view(ml_dtypes.float8_e4m3fn).astype(np.float64)
    else:
        nib = np.empty((g, 128, n, 4), np.uint8)
        nib[..., 0::2] = words & 0xF
        nib[..., 1::2] = words >> 4
        vals = E2M1[nib]
    vals = vals * np.repeat(np.exp2(scales.astype(np.float64) - 127.0), 8, axis=1)[..., None]
    return vals.transpose(0, 1, 3, 2).reshape(g * 512, n)


def sigmoid(v):
    return 1.0 / (1.0 + np.exp(-v))


D, E, T, I, G, U, Q = 512, 512, 4096, 1024, 64, 512, 128


def setup_inputs():
    n = np.random.standard_normal
    idx = np.random.permutation(T)[:I]
    idx2 = np.random.permutation(U)[:G]
    fd = mx_kscale(D)
    fe = mx_kscale(E)
    keysp = pack_weight(n((D, T)) / fd[:, None], "e4m3")
    valsp = pack_weight(n((E, T)) / fe[:, None], "e4m3")
    return {
        "query": (n((D, Q)) * 0.7 / np.sqrt(D) * fd[:, None]).astype(np.float32),
        "keys_words": keysp[0],
        "keys_scales": keysp[1],
        "ptab": (n((Q, U)) * 1.0).astype(np.float32),
        "gout": (n((E, Q)) * 1 / np.sqrt(E) * fe[:, None]).astype(np.float32),
        "vals_words": valsp[0],
        "vals_scales": valsp[1],
        "lam": (np.random.uniform(0.5, 1.5, (Q, 1))).astype(np.float32),
        "old": (0.5 * n((Q, U))).astype(np.float32),
        "offs": striped(idx),
        "offs2": striped(idx2),
    }


def reference(query, keys_words, keys_scales, ptab, gout, vals_words, vals_scales, lam, old, offs, offs2):
    idx = unstriped(offs)
    idx2 = unstriped(offs2)
    keysu = unpack_weight(keys_words, keys_scales, "e4m3")
    valsu = unpack_weight(vals_words, vals_scales, "e4m3")
    queryq = mxq(f64(query), 0, "e4m3")
    keysidxg = keysu[:, idx]
    a = queryq.T @ keysidxg
    b = a.reshape(Q, G, I // G).mean(axis=2)
    tp = f64(ptab)[:, idx2] * f64(lam)
    gt = sigmoid(tp + b)
    gr = np.repeat(gt, I // G, axis=1)
    r = np.exp(a - np.max(a, axis=1, keepdims=True))
    p = r * gr
    z = np.sum(p, axis=1, keepdims=True)
    goutq = mxq(f64(gout), 0, "e4m3")
    valsidxg = valsu[:, idx]
    c0 = goutq.T @ valsidxg
    dz = np.sum(p * c0, axis=1, keepdims=True) / np.square(z) * (-1.0)
    dp = 1.0 / z * c0 + dz
    dgr = dp * r
    dgt = dgr.reshape(Q, G, I // G).sum(axis=2)
    dtp = dgt * gt * (1.0 - gt)
    gs = dtp * f64(lam) * 64.0
    gf = np.zeros((Q, U))
    gf[:, idx2] = gs
    y = f64(old) + gf
    return y

@@ -1,0 +1,206 @@
+from contextlib import ExitStack
+
+import concourse.mybir as mybir
+from concourse.masks import make_identity
+
+D, E, T, I, G, U, Q = 512, 512, 4096, 1024, 64, 512, 128
+FLOPS = 2 * Q * I * (D + E)
+
+F32 = mybir.dt.float32
+BF16 = mybir.dt.bfloat16
+I32 = mybir.dt.int32
+U32 = mybir.dt.uint32
+U16 = mybir.dt.uint16
+U8 = mybir.dt.uint8
+FP8X4 = mybir.dt.float8_e4m3fn_x4
+ALU = mybir.AluOpType
+ACT = mybir.ActivationFunctionType
+AX = mybir.AxisListType
+
+P = 128
+PACK = 4
+HALF = 512
+PAGE = I // G
+RUN = PAGE // 2
+VROW = 4
+
+
+def tile_attend_bpagelift_kernel(tc, query, keys_words, keys_scales, ptab, gout, vals_words, vals_scales, lam, old, offs, offs2, out):
+    nc = tc.nc
+    with ExitStack() as ctx:
+        held = ctx.enter_context(tc.tile_pool(name="held", bufs=1))
+        psum = ctx.enter_context(tc.psum_pool(name="psum", bufs=1))
+
+        slots = held.tile([P, I // 16], U16, name="slots")
+        pages = held.tile([P, G // 16], U16, name="pages")
+        kw = held.tile([P, T], U32, name="kw", align_bytes=64)
+        vw = held.tile([P, T], U32, name="vw", align_bytes=64)
+        ks = held.tile([P, T], U8, name="ks", align_bytes=64)
+        vs = held.tile([P, T], U8, name="vs", align_bytes=64)
+        q_raw = held.tile([P, PACK, Q], F32, name="q_raw", tag="q_then_ptab")
+        g_raw = held.tile([P, PACK, Q], F32, name="g_raw", tag="g_then_old")
+        lam_sb = held.tile([P, 1], F32, name="lam_sb")
+        ident = held.tile([P, P], F32, name="ident")
+        gf = held.tile([P, U], F32, name="gf")
+        lift = held.tile([P, P], F32, name="lift")
+        seed = held.tile([P, 1], F32, name="seed")
+        warm = held.tile([P, 1], F32, name="warm")
+
+        nc.gpsimd.memset(seed[:], 0.0)
+        nc.scalar.activation(warm[:], seed[:], ACT.Exp)
+        nc.vector.memset(ks[:].bitcast(I32), 0)
+        nc.vector.memset(vs[:].bitcast(I32), 0)
+        nc.vector.memset(gf[:], 0.0)
+        nc.vector.memset(lift[:, G:], 0.0)
+
+        def load_scales(queue, plane, scales, first):
+            for r in range(4):
+                queue.dma_start(plane[first + r : P : 32, :].bitcast(I32), scales[0][r:16:4, :].bitcast(I32))
+
+        def load_words(tile, words):
+            nc.sync.dma_start(tile[:].bitcast(I32), words[0].rearrange("p n t -> p (n t)").bitcast(I32))
+
+        nc.sync.dma_start(slots[:], offs)
+        nc.sync.dma_start(q_raw[:], query.rearrange("(p j) w -> p j w", j=PACK))
+        nc.sync.dma_start(lam_sb[:], lam)
+        make_identity(nc, ident[:])
+        load_scales(nc.sync, ks, keys_scales, 0)
+        load_words(kw, keys_words)
+        load_scales(nc.scalar, vs, vals_scales, VROW)
+        nc.sync.dma_start(pages[:], offs2)
+        nc.sync.dma_start(g_raw[:], gout.rearrange("(p j) w -> p j w", j=PACK))
+        load_words(vw, vals_words)
+
+        def cast(raw, name):
+            grouped = held.tile([P, Q, PACK], BF16, name=name + "_bf", align_bytes=64)
+            nc.scalar.copy(grouped[:], raw[:].rearrange("p j w -> p w j"))
+            return grouped
+
+        def quantise(grouped, name):
+            codes = held.tile([P, Q], U32, name=name + "_codes", align_bytes=64)
+            plane = held.tile([P, Q], U8, name=name + "_plane", align_bytes=64)
+            nc.vector.quantize_mx(out=codes[:].bitcast(FP8X4), scales=plane[:], in_=grouped[:].rearrange("p w j -> p (w j)"))
+            return codes, plane
+
+        q_bf = cast(q_raw, "q")
+        ptab_sb = held.tile([P, U], F32, name="ptab_sb", tag="q_then_ptab")
+        nc.scalar.dma_start(ptab_sb[:], ptab)
+        lam64 = held.tile([P, 1], F32, name="lam64")
+        nc.scalar.activation(lam64[:], lam_sb[:], ACT.Copy, scale=-64.0)
+        g_bf = cast(g_raw, "g")
+        old_sb = held.tile([P, U], F32, name="old_sb", tag="g_then_old")
+        nc.sync.dma_start(old_sb[:], old)
+
+        ksg = held.tile([P, I], U8, name="ksg", align_bytes=64)
+        vsg = held.tile([P, I], U8, name="vsg", align_bytes=64)
+        nc.vector.tensor_copy(ksg[:], ks[:].indirect(slots[:]))
+        q_codes, q_plane = quantise(q_bf, "q")
+        nc.vector.tensor_copy(vsg[:], vs[:].indirect(slots[:]))
+
+        def half_list(h):
+            return slots[:, h * HALF // 16 : (h + 1) * HALF // 16]
+
+        def product(words, plane, first, codes, scales, name):
+            banks = []
+            for h in range(2):
+                picked = held.tile([P, HALF], U32, name=f"{name}_w{h}", tag=f"{name}_w{h}", align_bytes=64)
+                nc.vector.tensor_copy(picked[:], words[:].indirect(half_list(h)))
+                bank = psum.tile([P, HALF], F32, name=f"{name}_ps{h}")
+                nc.tensor.matmul_mx(
+                    out=bank[:],
+                    lhsT=codes[:].bitcast(FP8X4),
+                    lhsT_scale=scales[:],
+                    rhs=picked[:].bitcast(FP8X4),
+                    rhs_scale=plane[first:P, h * HALF : (h + 1) * HALF],
+                    start=True,
+                    stop=True,
+                )
+                banks.append(bank)
+            return banks
+
+        a_ps = product(kw, ksg, 0, q_codes, q_plane, "a")
+
+        lam16 = held.tile([P, G], F32, name="lam16", tag="a_w0", align_bytes=64)
+        nc.scalar.activation(lam16[:], lam_sb[:].to_broadcast([P, G]), ACT.Copy, scale=-float(PAGE))
+        neg_a = held.tile([P, RUN, 2, G], F32, name="neg_a")
+        low = [held.tile([P, 1], F32, name=f"low{h}") for h in range(2)]
+        GH = G // 2
+
+        def negate_and_min(h):
+            nc.vector.tensor_scalar(
+                neg_a[:, :, :, h * GH : (h + 1) * GH],
+                a_ps[h][:].rearrange("p (g u j) -> p j u g", u=2, j=RUN),
+                -1.0,
+                None if h == 0 else low[0][:],
+                ALU.mult,
+                ALU.min,
+                accum_out=low[h][:],
+            )
+
+        negate_and_min(0)
+        nc.vector.tensor_tensor(lift[:, :G], ptab_sb[:].indirect(pages[:]), lam16[:], ALU.mult)
+        negate_and_min(1)
+        g_codes, g_plane = quantise(g_bf, "g")
+
+        r = held.tile([P, I], F32, name="r")
+        for h in range(2):
+            nc.scalar.activation(r[:, h * HALF : (h + 1) * HALF], a_ps[h][:], ACT.Exp, bias=low[1][:], scale=1.0)
+
+        sums_t = psum.tile([P, P], F32, name="sums_t")
+        nc.tensor.matmul(sums_t[:], lift[:], ident[:], start=True, stop=False, is_transpose=True)
+        for j in range(RUN):
+            nc.tensor.matmul(
+                sums_t[:], neg_a[:, j, :, :].rearrange("p u g -> p (u g)"), ident[:], start=False, stop=(j == RUN - 1), is_transpose=True
+            )
+        sums_sb = held.tile([P, P], F32, name="sums_sb")
+        nc.scalar.copy(sums_sb[:], sums_t[:])
+        sums = psum.tile([P, P], F32, name="sums")
+        nc.tensor.transpose(sums[:], sums_sb[:], ident[:])
+
+        r_page = held.tile([P, G], F32, name="r_page")
+        for h in range(2):
+            nc.vector.tensor_reduce(
+                r_page[:, h * GH : (h + 1) * GH], r[:, h * HALF : (h + 1) * HALF].rearrange("p (g i) -> p g i", i=PAGE), AX.X, ALU.add
+            )
+        c_ps = product(vw, vsg, VROW, g_codes, g_plane, "c")
+
+        neg_x = held.tile([P, G], F32, name="neg_x", tag="c_w0", align_bytes=64)
+        nc.vector.tensor_reduce(neg_x[:], sums[:].rearrange("p (u g) -> p g u", u=2), AX.X, ALU.add)
+        gate = held.tile([P, G], F32, name="gate")
+        rest = held.tile([P, G], F32, name="rest")
+        nc.scalar.activation(gate[:], neg_x[:], ACT.Sigmoid, scale=-1.0 / PAGE)
+        nc.scalar.activation(rest[:], neg_x[:], ACT.Sigmoid, scale=1.0 / PAGE)
+
+
+        p_page = held.tile([P, G], F32, name="p_page")
+        z = held.tile([P, 1], F32, name="z")
+        nc.vector.scalar_tensor_tensor(p_page[:], gate[:], 1.0, r_page[:], ALU.mult, ALU.mult, accum_out=z[:])
+        slope = held.tile([P, G], F32, name="slope")
+        nc.vector.scalar_tensor_tensor(slope[:], gate[:], lam64[:], rest[:], ALU.mult, ALU.mult)
+        z_inv = held.tile([P, 1], F32, name="z_inv")
+        nc.vector.reciprocal(z_inv[:], z[:])
+        r_norm = held.tile([P, G], F32, name="r_norm")
+        nc.scalar.activation(r_norm[:], r_page[:], ACT.Copy, scale=z_inv[:])
+        weight = held.tile([P, G], F32, name="weight")
+        nc.scalar.activation(weight[:], slope[:], ACT.Copy, scale=z_inv[:])
+
+        rc = held.tile([P, I], F32, name="rc")
+        rc_page = held.tile([P, G], F32, name="rc_page")
+        for h in range(2):
+            cols = slice(h * HALF, (h + 1) * HALF)
+            nc.vector.tensor_tensor(rc[:, cols], c_ps[h][:], r[:, cols], ALU.mult)
+            nc.vector.tensor_reduce(rc_page[:, h * GH : (h + 1) * GH], rc[:, cols].rearrange("p (g i) -> p g i", i=PAGE), AX.X, ALU.add)
+
+        pc_page = held.tile([P, G], F32, name="pc_page")
+        total = held.tile([P, 1], F32, name="total")
+        nc.vector.scalar_tensor_tensor(pc_page[:], rc_page[:], 1.0, gate[:], ALU.mult, ALU.mult, accum_out=total[:])
+        neg_d = held.tile([P, G], F32, name="neg_d")
+        nc.vector.scalar_tensor_tensor(neg_d[:], r_norm[:], total[:], rc_page[:], ALU.mult, ALU.subtract)
+        nc.vector.tensor_tensor(gf[:].indirect(pages[:]), neg_d[:], weight[:], ALU.mult)
+
+        UH = U // 2
+        for h, queue in enumerate((nc.sync, nc.scalar)):
+            cols = slice(h * UH, (h + 1) * UH)
+            res = held.tile([P, UH], F32, name=f"res{h}")
+            nc.vector.tensor_tensor(res[:], gf[:, cols], old_sb[:, cols], ALU.add)
+            queue.dma_start(out[:, cols], res[:])

@@ -22,109 +22,114 @@ PACK = 4
 HALF = 512
 PAGE = I // G
 RUN = PAGE // 2
-VROW = 4
+GH = G // 2
+SPREAD = 8
 
 
 def tile_attend_bpagelift_kernel(tc, query, keys_words, keys_scales, ptab, gout, vals_words, vals_scales, lam, old, offs, offs2, out):
     nc = tc.nc
     with ExitStack() as ctx:
         held = ctx.enter_context(tc.tile_pool(name="held", bufs=1))
+        after_ks = ctx.enter_context(tc.tile_pool(name="after_ks", bufs=1))
+        after_vs = ctx.enter_context(tc.tile_pool(name="after_vs", bufs=1))
+        after_q = ctx.enter_context(tc.tile_pool(name="after_q", bufs=1))
         psum = ctx.enter_context(tc.psum_pool(name="psum", bufs=1))
 
         slots = held.tile([P, I // 16], U16, name="slots")
         pages = held.tile([P, G // 16], U16, name="pages")
         kw = held.tile([P, T], U32, name="kw", align_bytes=64)
-        vw = held.tile([P, T], U32, name="vw", align_bytes=64)
-        ks = held.tile([P, T], U8, name="ks", align_bytes=64)
-        vs = held.tile([P, T], U8, name="vs", align_bytes=64)
-        q_raw = held.tile([P, PACK, Q], F32, name="q_raw", tag="q_then_ptab")
-        g_raw = held.tile([P, PACK, Q], F32, name="g_raw", tag="g_then_old")
+        ks = after_ks.tile([P, T], U8, name="ks", offset=0, align_bytes=64)
+        vs = after_vs.tile([P, T], U8, name="vs", offset=0, align_bytes=64)
+        ks_plane = held.tile([P, I], U8, name="ks_plane", align_bytes=64)
+        vs_plane = held.tile([P, I], U8, name="vs_plane", align_bytes=64)
+        q_raw = held.tile([P, PACK, Q], F32, name="q_raw")
+        g_raw = held.tile([P, PACK, Q], F32, name="g_raw")
+        ptab_sb = held.tile([P, U], F32, name="ptab_sb")
         lam_sb = held.tile([P, 1], F32, name="lam_sb")
         ident = held.tile([P, P], F32, name="ident")
         gf = held.tile([P, U], F32, name="gf")
         lift = held.tile([P, P], F32, name="lift")
-        seed = held.tile([P, 1], F32, name="seed")
-        warm = held.tile([P, 1], F32, name="warm")
 
-        nc.gpsimd.memset(seed[:], 0.0)
-        nc.scalar.activation(warm[:], seed[:], ACT.Exp)
         nc.vector.memset(ks[:].bitcast(I32), 0)
         nc.vector.memset(vs[:].bitcast(I32), 0)
+        nc.vector.memset(ident[:], 0.0)
+        nc.vector.memset(ks_plane[:].bitcast(I32), 0)
+        nc.vector.memset(vs_plane[:].bitcast(I32), 0)
         nc.vector.memset(gf[:], 0.0)
         nc.vector.memset(lift[:, G:], 0.0)
+        make_identity(nc, ident[:], nomemset=True)
 
-        def load_scales(queue, plane, scales, first):
-            for r in range(4):
-                queue.dma_start(plane[first + r : P : 32, :].bitcast(I32), scales[0][r:16:4, :].bitcast(I32))
+        def load_scales(window, scales):
+            nc.scalar.dma_start(window[0:P:SPREAD, :].bitcast(I32), scales[0].bitcast(I32))
 
         def load_words(tile, words):
             nc.sync.dma_start(tile[:].bitcast(I32), words[0].rearrange("p n t -> p (n t)").bitcast(I32))
 
+        def load_rows(tile, rows):
+            nc.sync.dma_start(tile[:], rows.rearrange("(p j) w -> p j w", j=PACK))
+
         nc.sync.dma_start(slots[:], offs)
-        nc.sync.dma_start(q_raw[:], query.rearrange("(p j) w -> p j w", j=PACK))
+        load_rows(q_raw, query)
         nc.sync.dma_start(lam_sb[:], lam)
-        make_identity(nc, ident[:])
-        load_scales(nc.sync, ks, keys_scales, 0)
-        load_words(kw, keys_words)
-        load_scales(nc.scalar, vs, vals_scales, VROW)
         nc.sync.dma_start(pages[:], offs2)
-        nc.sync.dma_start(g_raw[:], gout.rearrange("(p j) w -> p j w", j=PACK))
-        load_words(vw, vals_words)
+        load_rows(g_raw, gout)
+        nc.sync.dma_start(ptab_sb[:], ptab)
+        load_words(kw, keys_words)
+        load_scales(ks, keys_scales)
+        load_scales(vs, vals_scales)
 
-        def cast(raw, name):
-            grouped = held.tile([P, Q, PACK], BF16, name=name + "_bf", align_bytes=64)
+        q_bf = after_q.tile([P, Q, PACK], BF16, name="q_bf", offset=I // 2, align_bytes=64)
+        g_bf = held.tile([P, Q, PACK], BF16, name="g_bf", align_bytes=64)
+        for grouped, raw in ((q_bf, q_raw), (g_bf, g_raw)):
             nc.scalar.copy(grouped[:], raw[:].rearrange("p j w -> p w j"))
-            return grouped
 
-        def quantise(grouped, name):
-            codes = held.tile([P, Q], U32, name=name + "_codes", align_bytes=64)
+        def gather_plane(window, picked, plane, queue):
+            nc.vector.tensor_copy(picked[:], window[:].indirect(slots[:]))
+            for first in range(0, P, 32):
+                queue.dma_start(plane[first : first + 4, :].bitcast(I32), picked[first : first + 32 : SPREAD, :].bitcast(I32))
+
+        def quantise(grouped, name, offset):
+            codes = after_ks.tile([P, Q], U32, name=name + "_codes", offset=offset, align_bytes=64)
             plane = held.tile([P, Q], U8, name=name + "_plane", align_bytes=64)
             nc.vector.quantize_mx(out=codes[:].bitcast(FP8X4), scales=plane[:], in_=grouped[:].rearrange("p w j -> p (w j)"))
             return codes, plane
 
-        q_bf = cast(q_raw, "q")
-        ptab_sb = held.tile([P, U], F32, name="ptab_sb", tag="q_then_ptab")
-        nc.scalar.dma_start(ptab_sb[:], ptab)
-        lam64 = held.tile([P, 1], F32, name="lam64")
-        nc.scalar.activation(lam64[:], lam_sb[:], ACT.Copy, scale=-64.0)
-        g_bf = cast(g_raw, "g")
-        old_sb = held.tile([P, U], F32, name="old_sb", tag="g_then_old")
-        nc.sync.dma_start(old_sb[:], old)
+        ks_picked = held.tile([P, I], U8, name="ks_picked", align_bytes=64)
+        gather_plane(ks, ks_picked, ks_plane, nc.sync)
+        q_mx = quantise(q_bf, "q", 0)
+        vw = after_q.tile([P, T], U32, name="vw", offset=I, align_bytes=64)
+        load_words(vw, vals_words)
+        vs_picked = after_q.tile([P, I], U8, name="vs_picked", offset=0, align_bytes=64)
+        gather_plane(vs, vs_picked, vs_plane, nc.scalar)
+        g_mx = quantise(g_bf, "g", 4 * Q)
 
-        ksg = held.tile([P, I], U8, name="ksg", align_bytes=64)
-        vsg = held.tile([P, I], U8, name="vsg", align_bytes=64)
-        nc.vector.tensor_copy(ksg[:], ks[:].indirect(slots[:]))
-        q_codes, q_plane = quantise(q_bf, "q")
-        nc.vector.tensor_copy(vsg[:], vs[:].indirect(slots[:]))
-
-        def half_list(h):
-            return slots[:, h * HALF // 16 : (h + 1) * HALF // 16]
-
-        def product(words, plane, first, codes, scales, name):
+        def product(words, plane, rows, name, pool):
             banks = []
             for h in range(2):
-                picked = held.tile([P, HALF], U32, name=f"{name}_w{h}", tag=f"{name}_w{h}", align_bytes=64)
-                nc.vector.tensor_copy(picked[:], words[:].indirect(half_list(h)))
+                picked = pool.tile([P, HALF], U32, name=f"{name}_w{h}", offset=4 * HALF * h, align_bytes=64)
+                nc.vector.tensor_copy(picked[:], words[:].indirect(slots[:, h * HALF // 16 : (h + 1) * HALF // 16]))
                 bank = psum.tile([P, HALF], F32, name=f"{name}_ps{h}")
                 nc.tensor.matmul_mx(
                     out=bank[:],
-                    lhsT=codes[:].bitcast(FP8X4),
-                    lhsT_scale=scales[:],
+                    lhsT=rows[0][:].bitcast(FP8X4),
+                    lhsT_scale=rows[1][:],
                     rhs=picked[:].bitcast(FP8X4),
-                    rhs_scale=plane[first:P, h * HALF : (h + 1) * HALF],
+                    rhs_scale=plane[:, h * HALF : (h + 1) * HALF],
                     start=True,
                     stop=True,
                 )
                 banks.append(bank)
             return banks
 
-        a_ps = product(kw, ksg, 0, q_codes, q_plane, "a")
+        a_ps = product(kw, ks_plane, q_mx, "a", after_vs)
 
-        lam16 = held.tile([P, G], F32, name="lam16", tag="a_w0", align_bytes=64)
+        lam16 = after_vs.tile([P, G], F32, name="lam16", offset=0, align_bytes=64)
         nc.scalar.activation(lam16[:], lam_sb[:].to_broadcast([P, G]), ACT.Copy, scale=-float(PAGE))
+        old_sb = after_vs.tile([P, U], F32, name="old_sb", offset=4 * HALF, align_bytes=64)
+        nc.sync.dma_start(old_sb[:], old)
+
         neg_a = held.tile([P, RUN, 2, G], F32, name="neg_a")
         low = [held.tile([P, 1], F32, name=f"low{h}") for h in range(2)]
-        GH = G // 2
 
         def negate_and_min(h):
             nc.vector.tensor_scalar(
@@ -140,7 +145,6 @@ def tile_attend_bpagelift_kernel(tc, query, keys_words, keys_scales, ptab, gout,
         negate_and_min(0)
         nc.vector.tensor_tensor(lift[:, :G], ptab_sb[:].indirect(pages[:]), lam16[:], ALU.mult)
         negate_and_min(1)
-        g_codes, g_plane = quantise(g_bf, "g")
 
         r = held.tile([P, I], F32, name="r")
         for h in range(2):
@@ -162,27 +166,28 @@ def tile_attend_bpagelift_kernel(tc, query, keys_words, keys_scales, ptab, gout,
             nc.vector.tensor_reduce(
                 r_page[:, h * GH : (h + 1) * GH], r[:, h * HALF : (h + 1) * HALF].rearrange("p (g i) -> p g i", i=PAGE), AX.X, ALU.add
             )
-        c_ps = product(vw, vsg, VROW, g_codes, g_plane, "c")
 
-        neg_x = held.tile([P, G], F32, name="neg_x", tag="c_w0", align_bytes=64)
+        after_c = ctx.enter_context(tc.tile_pool(name="after_c", bufs=1))
+        c_ps = product(vw, vs_plane, g_mx, "c", after_c)
+
+        neg_x = after_c.tile([P, G], F32, name="neg_x", offset=0, align_bytes=64)
         nc.vector.tensor_reduce(neg_x[:], sums[:].rearrange("p (u g) -> p g u", u=2), AX.X, ALU.add)
         gate = held.tile([P, G], F32, name="gate")
         rest = held.tile([P, G], F32, name="rest")
         nc.scalar.activation(gate[:], neg_x[:], ACT.Sigmoid, scale=-1.0 / PAGE)
         nc.scalar.activation(rest[:], neg_x[:], ACT.Sigmoid, scale=1.0 / PAGE)
 
-
         p_page = held.tile([P, G], F32, name="p_page")
-        z = held.tile([P, 1], F32, name="z")
-        nc.vector.scalar_tensor_tensor(p_page[:], gate[:], 1.0, r_page[:], ALU.mult, ALU.mult, accum_out=z[:])
+        z4 = held.tile([P, 1], F32, name="z4")
+        nc.vector.scalar_tensor_tensor(p_page[:], gate[:], 0.25, r_page[:], ALU.mult, ALU.mult, accum_out=z4[:])
         slope = held.tile([P, G], F32, name="slope")
-        nc.vector.scalar_tensor_tensor(slope[:], gate[:], lam64[:], rest[:], ALU.mult, ALU.mult)
-        z_inv = held.tile([P, 1], F32, name="z_inv")
-        nc.vector.reciprocal(z_inv[:], z[:])
+        nc.vector.scalar_tensor_tensor(slope[:], gate[:], lam16[:, 0:1], rest[:], ALU.mult, ALU.mult)
+        z4_inv = held.tile([P, 1], F32, name="z4_inv")
+        nc.vector.reciprocal(z4_inv[:], z4[:])
         r_norm = held.tile([P, G], F32, name="r_norm")
-        nc.scalar.activation(r_norm[:], r_page[:], ACT.Copy, scale=z_inv[:])
+        nc.scalar.activation(r_norm[:], r_page[:], ACT.Copy, scale=z4_inv[:])
         weight = held.tile([P, G], F32, name="weight")
-        nc.scalar.activation(weight[:], slope[:], ACT.Copy, scale=z_inv[:])
+        nc.scalar.activation(weight[:], slope[:], ACT.Copy, scale=z4_inv[:])
 
         rc = held.tile([P, I], F32, name="rc")
         rc_page = held.tile([P, G], F32, name="rc_page")
@@ -192,10 +197,10 @@ def tile_attend_bpagelift_kernel(tc, query, keys_words, keys_scales, ptab, gout,
             nc.vector.tensor_reduce(rc_page[:, h * GH : (h + 1) * GH], rc[:, cols].rearrange("p (g i) -> p g i", i=PAGE), AX.X, ALU.add)
 
         pc_page = held.tile([P, G], F32, name="pc_page")
-        total = held.tile([P, 1], F32, name="total")
-        nc.vector.scalar_tensor_tensor(pc_page[:], rc_page[:], 1.0, gate[:], ALU.mult, ALU.mult, accum_out=total[:])
+        total4 = held.tile([P, 1], F32, name="total4")
+        nc.vector.scalar_tensor_tensor(pc_page[:], rc_page[:], 0.25, gate[:], ALU.mult, ALU.mult, accum_out=total4[:])
         neg_d = held.tile([P, G], F32, name="neg_d")
-        nc.vector.scalar_tensor_tensor(neg_d[:], r_norm[:], total[:], rc_page[:], ALU.mult, ALU.subtract)
+        nc.vector.scalar_tensor_tensor(neg_d[:], r_norm[:], total4[:], rc_page[:], ALU.mult, ALU.subtract)
         nc.vector.tensor_tensor(gf[:].indirect(pages[:]), neg_d[:], weight[:], ALU.mult)
 
         UH = U // 2

@@ -23,7 +23,9 @@ HALF = 512
 PAGE = I // G
 RUN = PAGE // 2
 GH = G // 2
-SPREAD = 8
+ROWS = 16
+KS_ROW = 112
+VS_ROW = 48
 
 
 def tile_attend_bpagelift_kernel(tc, query, keys_words, keys_scales, ptab, gout, vals_words, vals_scales, lam, old, offs, offs2, out):
@@ -47,20 +49,18 @@ def tile_attend_bpagelift_kernel(tc, query, keys_words, keys_scales, ptab, gout,
         ptab_sb = held.tile([P, U], F32, name="ptab_sb")
         lam_sb = held.tile([P, 1], F32, name="lam_sb")
         ident = held.tile([P, P], F32, name="ident")
-        gf = held.tile([P, U], F32, name="gf")
         lift = held.tile([P, P], F32, name="lift")
 
-        nc.vector.memset(ks[:].bitcast(I32), 0)
-        nc.vector.memset(vs[:].bitcast(I32), 0)
-        nc.vector.memset(ident[:], 0.0)
-        nc.vector.memset(ks_plane[:].bitcast(I32), 0)
-        nc.vector.memset(vs_plane[:].bitcast(I32), 0)
-        nc.vector.memset(gf[:], 0.0)
-        nc.vector.memset(lift[:, G:], 0.0)
-        make_identity(nc, ident[:], nomemset=True)
+        nc.vector.memset(ks[:KS_ROW, :].bitcast(I32), 0)
+        nc.vector.memset(vs[:VS_ROW, :].bitcast(I32), 0)
+        nc.vector.memset(vs[VS_ROW + ROWS :, :].bitcast(I32), 0)
+        make_identity(nc, ident[:])
+        nc.gpsimd.memset(ks_plane[:].bitcast(I32), 0)
+        nc.gpsimd.memset(vs_plane[:].bitcast(I32), 0)
+        nc.gpsimd.memset(lift[:, G:], 0.0)
 
-        def load_scales(window, scales):
-            nc.scalar.dma_start(window[0:P:SPREAD, :].bitcast(I32), scales[0].bitcast(I32))
+        def load_scales(window, first, scales):
+            nc.sync.dma_start(window[first : first + ROWS, :].bitcast(I32), scales[0].bitcast(I32))
 
         def load_words(tile, words):
             nc.sync.dma_start(tile[:].bitcast(I32), words[0].rearrange("p n t -> p (n t)").bitcast(I32))
@@ -69,24 +69,25 @@ def tile_attend_bpagelift_kernel(tc, query, keys_words, keys_scales, ptab, gout,
             nc.sync.dma_start(tile[:], rows.rearrange("(p j) w -> p j w", j=PACK))
 
         nc.sync.dma_start(slots[:], offs)
+        load_scales(ks, KS_ROW, keys_scales)
+        load_scales(vs, VS_ROW, vals_scales)
         load_rows(q_raw, query)
         nc.sync.dma_start(lam_sb[:], lam)
         nc.sync.dma_start(pages[:], offs2)
+        load_words(kw, keys_words)
         load_rows(g_raw, gout)
         nc.sync.dma_start(ptab_sb[:], ptab)
-        load_words(kw, keys_words)
-        load_scales(ks, keys_scales)
-        load_scales(vs, vals_scales)
 
         q_bf = after_q.tile([P, Q, PACK], BF16, name="q_bf", offset=I // 2, align_bytes=64)
         g_bf = held.tile([P, Q, PACK], BF16, name="g_bf", align_bytes=64)
         for grouped, raw in ((q_bf, q_raw), (g_bf, g_raw)):
             nc.scalar.copy(grouped[:], raw[:].rearrange("p j w -> p w j"))
 
-        def gather_plane(window, picked, plane, queue):
+        def gather_plane(window, first, picked, plane):
             nc.vector.tensor_copy(picked[:], window[:].indirect(slots[:]))
-            for first in range(0, P, 32):
-                queue.dma_start(plane[first : first + 4, :].bitcast(I32), picked[first : first + 32 : SPREAD, :].bitcast(I32))
+            for quad in range(4):
+                rows = picked[first + 4 * quad : first + 4 * quad + 4, :]
+                nc.sync.dma_start(plane[32 * quad : 32 * quad + 4, :].bitcast(I32), rows.bitcast(I32))
 
         def quantise(grouped, name, offset):
             codes = after_ks.tile([P, Q], U32, name=name + "_codes", offset=offset, align_bytes=64)
@@ -95,12 +96,12 @@ def tile_attend_bpagelift_kernel(tc, query, keys_words, keys_scales, ptab, gout,
             return codes, plane
 
         ks_picked = held.tile([P, I], U8, name="ks_picked", align_bytes=64)
-        gather_plane(ks, ks_picked, ks_plane, nc.sync)
+        gather_plane(ks, KS_ROW, ks_picked, ks_plane)
         q_mx = quantise(q_bf, "q", 0)
         vw = after_q.tile([P, T], U32, name="vw", offset=I, align_bytes=64)
         load_words(vw, vals_words)
         vs_picked = after_q.tile([P, I], U8, name="vs_picked", offset=0, align_bytes=64)
-        gather_plane(vs, vs_picked, vs_plane, nc.scalar)
+        gather_plane(vs, VS_ROW, vs_picked, vs_plane)
         g_mx = quantise(g_bf, "g", 4 * Q)
 
         def product(words, plane, rows, name, pool):
@@ -125,7 +126,7 @@ def tile_attend_bpagelift_kernel(tc, query, keys_words, keys_scales, ptab, gout,
 
         lam16 = after_vs.tile([P, G], F32, name="lam16", offset=0, align_bytes=64)
         nc.scalar.activation(lam16[:], lam_sb[:].to_broadcast([P, G]), ACT.Copy, scale=-float(PAGE))
-        old_sb = after_vs.tile([P, U], F32, name="old_sb", offset=4 * HALF, align_bytes=64)
+        old_sb = after_vs.tile([P, U], F32, name="old_sb", offset=5 * HALF, align_bytes=64)
         nc.sync.dma_start(old_sb[:], old)
 
         neg_a = held.tile([P, RUN, 2, G], F32, name="neg_a")
@@ -145,6 +146,8 @@ def tile_attend_bpagelift_kernel(tc, query, keys_words, keys_scales, ptab, gout,
         negate_and_min(0)
         nc.vector.tensor_tensor(lift[:, :G], ptab_sb[:].indirect(pages[:]), lam16[:], ALU.mult)
         negate_and_min(1)
+        gf = after_vs.tile([P, U], F32, name="gf", offset=HALF, align_bytes=64)
+        nc.vector.memset(gf[:], 0.0)
 
         r = held.tile([P, I], F32, name="r")
         for h in range(2):

@@ -53,11 +53,11 @@ def tile_attend_bpagelift_kernel(tc, query, keys_words, keys_scales, ptab, gout,
 
         nc.vector.memset(ks[:KS_ROW, :].bitcast(I32), 0)
         nc.vector.memset(vs[:VS_ROW, :].bitcast(I32), 0)
-        nc.vector.memset(vs[VS_ROW + ROWS :, :].bitcast(I32), 0)
+        gf = held.tile([P, U], F32, name="gf")
+        nc.vector.memset(gf[:], 0.0)
         make_identity(nc, ident[:])
-        nc.gpsimd.memset(ks_plane[:].bitcast(I32), 0)
-        nc.gpsimd.memset(vs_plane[:].bitcast(I32), 0)
         nc.gpsimd.memset(lift[:, G:], 0.0)
+        nc.gpsimd.memset(vs[VS_ROW + ROWS :, :].bitcast(I32), 0)
 
         def load_scales(window, first, scales):
             nc.sync.dma_start(window[first : first + ROWS, :].bitcast(I32), scales[0].bitcast(I32))
@@ -68,8 +68,8 @@ def tile_attend_bpagelift_kernel(tc, query, keys_words, keys_scales, ptab, gout,
         def load_rows(tile, rows):
             nc.sync.dma_start(tile[:], rows.rearrange("(p j) w -> p j w", j=PACK))
 
-        nc.sync.dma_start(slots[:], offs)
         load_scales(ks, KS_ROW, keys_scales)
+        nc.sync.dma_start(slots[:], offs)
         load_scales(vs, VS_ROW, vals_scales)
         load_rows(q_raw, query)
         nc.sync.dma_start(lam_sb[:], lam)
@@ -146,12 +146,12 @@ def tile_attend_bpagelift_kernel(tc, query, keys_words, keys_scales, ptab, gout,
         negate_and_min(0)
         nc.vector.tensor_tensor(lift[:, :G], ptab_sb[:].indirect(pages[:]), lam16[:], ALU.mult)
         negate_and_min(1)
-        gf = after_vs.tile([P, U], F32, name="gf", offset=HALF, align_bytes=64)
-        nc.vector.memset(gf[:], 0.0)
 
         r = held.tile([P, I], F32, name="r")
         for h in range(2):
-            nc.scalar.activation(r[:, h * HALF : (h + 1) * HALF], a_ps[h][:], ACT.Exp, bias=low[1][:], scale=1.0)
+            nc.scalar.activation(r[:, h * HALF : (h + 1) * HALF], a_ps[h][:], ACT.Exp, bias=low[h][:], scale=1.0)
+        shrink = held.tile([P, 1], F32, name="shrink")
+        nc.scalar.activation(shrink[:], low[0][:], ACT.Exp, bias=low[1][:], scale=-1.0)
 
         sums_t = psum.tile([P, P], F32, name="sums_t")
         nc.tensor.matmul(sums_t[:], lift[:], ident[:], start=True, stop=False, is_transpose=True)
@@ -178,6 +178,7 @@ def tile_attend_bpagelift_kernel(tc, query, keys_words, keys_scales, ptab, gout,
         gate = held.tile([P, G], F32, name="gate")
         rest = held.tile([P, G], F32, name="rest")
         nc.scalar.activation(gate[:], neg_x[:], ACT.Sigmoid, scale=-1.0 / PAGE)
+        nc.scalar.activation(gate[:, :GH], gate[:, :GH], ACT.Copy, scale=shrink[:])
         nc.scalar.activation(rest[:], neg_x[:], ACT.Sigmoid, scale=1.0 / PAGE)
 
         p_page = held.tile([P, G], F32, name="p_page")

from contextlib import ExitStack

import concourse.mybir as mybir
from concourse.masks import make_identity

D, E, T, I, G, U, Q = 512, 512, 4096, 1024, 64, 512, 128
FLOPS = 2 * Q * I * (D + E)

F32 = mybir.dt.float32
BF16 = mybir.dt.bfloat16
I32 = mybir.dt.int32
U32 = mybir.dt.uint32
U16 = mybir.dt.uint16
U8 = mybir.dt.uint8
FP8X4 = mybir.dt.float8_e4m3fn_x4
ALU = mybir.AluOpType
ACT = mybir.ActivationFunctionType
AX = mybir.AxisListType

P = 128
PACK = 4
HALF = 512
PAGE = I // G
RUN = PAGE // 2
GH = G // 2
ROWS = 16
KS_ROW = 112
VS_ROW = 48


def tile_attend_bpagelift_kernel(tc, query, keys_words, keys_scales, ptab, gout, vals_words, vals_scales, lam, old, offs, offs2, out):
    nc = tc.nc
    with ExitStack() as ctx:
        held = ctx.enter_context(tc.tile_pool(name="held", bufs=1))
        after_ks = ctx.enter_context(tc.tile_pool(name="after_ks", bufs=1))
        after_vs = ctx.enter_context(tc.tile_pool(name="after_vs", bufs=1))
        after_q = ctx.enter_context(tc.tile_pool(name="after_q", bufs=1))
        psum = ctx.enter_context(tc.psum_pool(name="psum", bufs=1))

        slots = held.tile([P, I // 16], U16, name="slots")
        pages = held.tile([P, G // 16], U16, name="pages")
        kw = held.tile([P, T], U32, name="kw", align_bytes=64)
        ks = after_ks.tile([P, T], U8, name="ks", offset=0, align_bytes=64)
        vs = after_vs.tile([P, T], U8, name="vs", offset=0, align_bytes=64)
        ks_plane = held.tile([P, I], U8, name="ks_plane", align_bytes=64)
        vs_plane = held.tile([P, I], U8, name="vs_plane", align_bytes=64)
        q_raw = held.tile([P, PACK, Q], F32, name="q_raw")
        g_raw = held.tile([P, PACK, Q], F32, name="g_raw")
        ptab_sb = held.tile([P, U], F32, name="ptab_sb")
        lam_sb = held.tile([P, 1], F32, name="lam_sb")
        ident = held.tile([P, P], F32, name="ident")
        lift = held.tile([P, P], F32, name="lift")

        nc.vector.memset(ks[:KS_ROW, :].bitcast(I32), 0)
        nc.vector.memset(vs[:VS_ROW, :].bitcast(I32), 0)
        gf = held.tile([P, U], F32, name="gf")
        nc.vector.memset(gf[:], 0.0)
        make_identity(nc, ident[:])
        nc.gpsimd.memset(lift[:, G:], 0.0)
        nc.gpsimd.memset(vs[VS_ROW + ROWS :, :].bitcast(I32), 0)

        def load_scales(window, first, scales):
            nc.sync.dma_start(window[first : first + ROWS, :].bitcast(I32), scales[0].bitcast(I32))

        def load_words(tile, words):
            nc.sync.dma_start(tile[:].bitcast(I32), words[0].rearrange("p n t -> p (n t)").bitcast(I32))

        def load_rows(tile, rows):
            nc.sync.dma_start(tile[:], rows.rearrange("(p j) w -> p j w", j=PACK))

        load_scales(ks, KS_ROW, keys_scales)
        nc.sync.dma_start(slots[:], offs)
        load_scales(vs, VS_ROW, vals_scales)
        load_rows(q_raw, query)
        nc.sync.dma_start(lam_sb[:], lam)
        nc.sync.dma_start(pages[:], offs2)
        load_words(kw, keys_words)
        load_rows(g_raw, gout)
        nc.sync.dma_start(ptab_sb[:], ptab)

        q_bf = after_q.tile([P, Q, PACK], BF16, name="q_bf", offset=I // 2, align_bytes=64)
        g_bf = held.tile([P, Q, PACK], BF16, name="g_bf", align_bytes=64)
        for grouped, raw in ((q_bf, q_raw), (g_bf, g_raw)):
            nc.scalar.copy(grouped[:], raw[:].rearrange("p j w -> p w j"))

        def gather_plane(window, first, picked, plane):
            nc.vector.tensor_copy(picked[:], window[:].indirect(slots[:]))
            for quad in range(4):
                rows = picked[first + 4 * quad : first + 4 * quad + 4, :]
                nc.sync.dma_start(plane[32 * quad : 32 * quad + 4, :].bitcast(I32), rows.bitcast(I32))

        def quantise(grouped, name, offset):
            codes = after_ks.tile([P, Q], U32, name=name + "_codes", offset=offset, align_bytes=64)
            plane = held.tile([P, Q], U8, name=name + "_plane", align_bytes=64)
            nc.vector.quantize_mx(out=codes[:].bitcast(FP8X4), scales=plane[:], in_=grouped[:].rearrange("p w j -> p (w j)"))
            return codes, plane

        ks_picked = held.tile([P, I], U8, name="ks_picked", align_bytes=64)
        gather_plane(ks, KS_ROW, ks_picked, ks_plane)
        q_mx = quantise(q_bf, "q", 0)
        vw = after_q.tile([P, T], U32, name="vw", offset=I, align_bytes=64)
        load_words(vw, vals_words)
        vs_picked = after_q.tile([P, I], U8, name="vs_picked", offset=0, align_bytes=64)
        gather_plane(vs, VS_ROW, vs_picked, vs_plane)
        g_mx = quantise(g_bf, "g", 4 * Q)

        def product(words, plane, rows, name, pool):
            banks = []
            for h in range(2):
                picked = pool.tile([P, HALF], U32, name=f"{name}_w{h}", offset=4 * HALF * h, align_bytes=64)
                nc.vector.tensor_copy(picked[:], words[:].indirect(slots[:, h * HALF // 16 : (h + 1) * HALF // 16]))
                bank = psum.tile([P, HALF], F32, name=f"{name}_ps{h}")
                nc.tensor.matmul_mx(
                    out=bank[:],
                    lhsT=rows[0][:].bitcast(FP8X4),
                    lhsT_scale=rows[1][:],
                    rhs=picked[:].bitcast(FP8X4),
                    rhs_scale=plane[:, h * HALF : (h + 1) * HALF],
                    start=True,
                    stop=True,
                )
                banks.append(bank)
            return banks

        a_ps = product(kw, ks_plane, q_mx, "a", after_vs)

        lam16 = after_vs.tile([P, G], F32, name="lam16", offset=0, align_bytes=64)
        nc.scalar.activation(lam16[:], lam_sb[:].to_broadcast([P, G]), ACT.Copy, scale=-float(PAGE))
        old_sb = after_vs.tile([P, U], F32, name="old_sb", offset=5 * HALF, align_bytes=64)
        nc.sync.dma_start(old_sb[:], old)

        neg_a = held.tile([P, RUN, 2, G], F32, name="neg_a")
        low = [held.tile([P, 1], F32, name=f"low{h}") for h in range(2)]

        def negate_and_min(h):
            nc.vector.tensor_scalar(
                neg_a[:, :, :, h * GH : (h + 1) * GH],
                a_ps[h][:].rearrange("p (g u j) -> p j u g", u=2, j=RUN),
                -1.0,
                None if h == 0 else low[0][:],
                ALU.mult,
                ALU.min,
                accum_out=low[h][:],
            )

        negate_and_min(0)
        nc.vector.tensor_tensor(lift[:, :G], ptab_sb[:].indirect(pages[:]), lam16[:], ALU.mult)
        negate_and_min(1)

        r = held.tile([P, I], F32, name="r")
        for h in range(2):
            nc.scalar.activation(r[:, h * HALF : (h + 1) * HALF], a_ps[h][:], ACT.Exp, bias=low[h][:], scale=1.0)
        shrink = held.tile([P, 1], F32, name="shrink")
        nc.scalar.activation(shrink[:], low[0][:], ACT.Exp, bias=low[1][:], scale=-1.0)

        sums_t = psum.tile([P, P], F32, name="sums_t")
        nc.tensor.matmul(sums_t[:], lift[:], ident[:], start=True, stop=False, is_transpose=True)
        for j in range(RUN):
            nc.tensor.matmul(
                sums_t[:], neg_a[:, j, :, :].rearrange("p u g -> p (u g)"), ident[:], start=False, stop=(j == RUN - 1), is_transpose=True
            )
        sums_sb = held.tile([P, P], F32, name="sums_sb")
        nc.scalar.copy(sums_sb[:], sums_t[:])
        sums = psum.tile([P, P], F32, name="sums")
        nc.tensor.transpose(sums[:], sums_sb[:], ident[:])

        r_page = held.tile([P, G], F32, name="r_page")
        for h in range(2):
            nc.vector.tensor_reduce(
                r_page[:, h * GH : (h + 1) * GH], r[:, h * HALF : (h + 1) * HALF].rearrange("p (g i) -> p g i", i=PAGE), AX.X, ALU.add
            )

        after_c = ctx.enter_context(tc.tile_pool(name="after_c", bufs=1))
        c_ps = product(vw, vs_plane, g_mx, "c", after_c)

        neg_x = after_c.tile([P, G], F32, name="neg_x", offset=0, align_bytes=64)
        nc.vector.tensor_reduce(neg_x[:], sums[:].rearrange("p (u g) -> p g u", u=2), AX.X, ALU.add)
        gate = held.tile([P, G], F32, name="gate")
        rest = held.tile([P, G], F32, name="rest")
        nc.scalar.activation(gate[:], neg_x[:], ACT.Sigmoid, scale=-1.0 / PAGE)
        nc.scalar.activation(gate[:, :GH], gate[:, :GH], ACT.Copy, scale=shrink[:])
        nc.scalar.activation(rest[:], neg_x[:], ACT.Sigmoid, scale=1.0 / PAGE)

        p_page = held.tile([P, G], F32, name="p_page")
        z4 = held.tile([P, 1], F32, name="z4")
        nc.vector.scalar_tensor_tensor(p_page[:], gate[:], 0.25, r_page[:], ALU.mult, ALU.mult, accum_out=z4[:])
        slope = held.tile([P, G], F32, name="slope")
        nc.vector.scalar_tensor_tensor(slope[:], gate[:], lam16[:, 0:1], rest[:], ALU.mult, ALU.mult)
        z4_inv = held.tile([P, 1], F32, name="z4_inv")
        nc.vector.reciprocal(z4_inv[:], z4[:])
        r_norm = held.tile([P, G], F32, name="r_norm")
        nc.scalar.activation(r_norm[:], r_page[:], ACT.Copy, scale=z4_inv[:])
        weight = held.tile([P, G], F32, name="weight")
        nc.scalar.activation(weight[:], slope[:], ACT.Copy, scale=z4_inv[:])

        rc = held.tile([P, I], F32, name="rc")
        rc_page = held.tile([P, G], F32, name="rc_page")
        for h in range(2):
            cols = slice(h * HALF, (h + 1) * HALF)
            nc.vector.tensor_tensor(rc[:, cols], c_ps[h][:], r[:, cols], ALU.mult)
            nc.vector.tensor_reduce(rc_page[:, h * GH : (h + 1) * GH], rc[:, cols].rearrange("p (g i) -> p g i", i=PAGE), AX.X, ALU.add)

        pc_page = held.tile([P, G], F32, name="pc_page")
        total4 = held.tile([P, 1], F32, name="total4")
        nc.vector.scalar_tensor_tensor(pc_page[:], rc_page[:], 0.25, gate[:], ALU.mult, ALU.mult, accum_out=total4[:])
        neg_d = held.tile([P, G], F32, name="neg_d")
        nc.vector.scalar_tensor_tensor(neg_d[:], r_norm[:], total4[:], rc_page[:], ALU.mult, ALU.subtract)
        nc.vector.tensor_tensor(gf[:].indirect(pages[:]), neg_d[:], weight[:], ALU.mult)

        UH = U // 2
        for h, queue in enumerate((nc.sync, nc.scalar)):
            cols = slice(h * UH, (h + 1) * UH)
            res = held.tile([P, UH], F32, name=f"res{h}")
            nc.vector.tensor_tensor(res[:], gf[:, cols], old_sb[:, cols], ALU.add)
            queue.dma_start(out[:, cols], res[:])
